import numpy as np
import ml_dtypes


def mxq(x, axis, fmt="e4m3"):
    dtype, down = {"e4m3": (ml_dtypes.float8_e4m3fn, 7), "e5m2": (ml_dtypes.float8_e5m2, 14)}[fmt]
    v = np.moveaxis(np.asarray(x, np.float32).astype(ml_dtypes.bfloat16).astype(np.float64), axis, -1)
    blocks = v.reshape(v.shape[:-1] + (-1, 32))
    amax = np.abs(blocks).max(-1, keepdims=True)
    byte = np.maximum(np.where(amax > 0, np.frexp(amax)[1] - 1 + 127, 0) - down, 1)
    scale = np.exp2(byte - 127.0)
    codes = (blocks / scale).astype(np.float32).astype(dtype).astype(np.float64)
    return np.moveaxis((codes * scale).reshape(v.shape), -1, axis)


WIDE = False


def mx_kscale(k):
    if not WIDE:
        return np.ones(k)
    levels = np.array([10, -10, 5, -5, 0])
    if k % 512:
        return np.exp2(np.random.permutation(np.resize(levels, k // 32))).repeat(32)
    a = np.empty((k // 512, 16))
    for p in range(k // 512):
        a[p, :8] = np.random.permutation(np.resize(levels, 8))
        for g in range(8):
            far = levels[np.abs(levels - a[p, g]) >= 10]
            a[p, g + 8] = far[np.random.randint(len(far))]
    return np.exp2(a.ravel()).repeat(32)


def f64(x):
    return np.asarray(x).astype(np.float64)


def striped(idx):
    return np.tile(idx.reshape(-1, 16).T, (8, 1)).astype(np.uint16)


def unstriped(offs):
    return offs[:16].T.reshape(-1).astype(np.int64)


def striped8(idx):
    return np.concatenate([x.reshape(-1, 16).T for x in idx]).astype(np.uint16)


def runs(offs, k):
    lists = np.stack([offs[16 * r : 16 * r + 16].T.reshape(-1) for r in range(8)]).astype(np.int64)
    return lists[np.arange(k) % 512 // 64]


def pack_weight(w):
    k, n = w.shape
    w = f64(np.asarray(w, np.float32).astype(ml_dtypes.bfloat16)).reshape(k // 32, 32, n)
    amax = np.abs(w).max(1)
    byte = np.clip(np.where(amax > 0, np.frexp(amax)[1] - 1 + 127 - 7, 1), 1, 254)
    scaled = (w * np.exp2(127.0 - byte)[:, None, :]).reshape(k, n).astype(np.float32)
    words = np.ascontiguousarray(scaled.reshape(k // 512, 128, 4, n).transpose(0, 1, 3, 2)).astype(ml_dtypes.float8_e4m3fn).view(np.uint8)
    return words, np.ascontiguousarray(byte.astype(np.uint8).reshape(k // 512, 16, n))


def unpack_weight(words, scales):
    g, p, n, _ = words.shape
    vals = np.ascontiguousarray(words).view(ml_dtypes.float8_e4m3fn).astype(np.float64) * np.repeat(np.exp2(scales.astype(np.float64) - 127.0), 8, axis=1)[..., None]
    return vals.transpose(0, 1, 3, 2).reshape(g * 512, n)


def relu(v):
    return np.maximum(v, 0.0)


K, T, S, G, H, W, C = 512, 1024, 256, 2048, 512, 128, 512


def setup_inputs():
    n = np.random.standard_normal
    s = mx_kscale(K)[:, None]
    packed_xT = pack_weight(n((K, T)) * s)
    packed_dT = pack_weight(n((K, G)) / s)
    return {
        "x_words": packed_xT[0],
        "x_scales": packed_xT[1],
        "d_words": packed_dT[0],
        "d_scales": packed_dT[1],
        "gs": (np.random.uniform(0.5, 1.5, (K, 1)) / s).astype(np.float32),
        "offs": striped(np.random.permutation(T)[:S]),
        "ka": striped8(np.random.randint(0, G, (8, H))),
        "kb": striped8(np.random.randint(0, G, (8, H))),
        "n1": striped(np.random.permutation(S)[:W]),
        "n2": striped(np.random.permutation(S)[:W]),
        "n3": striped(np.random.permutation(S)),
        "cand": striped(np.random.permutation(T)[:C]),
        "n4": striped(np.random.permutation(S)),
    }


def reference(x_words, x_scales, d_words, d_scales, gs, offs, ka, kb, n1, n2, n3, cand, n4):
    x_cand = unpack_weight(x_words, x_scales)[:, unstriped(cand)]
    d_ka = unpack_weight(d_words, d_scales)[np.arange(K)[:, None], runs(ka, K)]
    xq = unpack_weight(x_words, x_scales)[:, unstriped(offs)]
    d_kb = unpack_weight(d_words, d_scales)[np.arange(K)[:, None], runs(kb, K)]
    h = 0.0625 * (d_ka.T @ xq + d_kb.T @ xq)
    pa = h[:, unstriped(n2)]
    ds = h.copy()
    ds[:, unstriped(n1)] = pa
    z = f64(gs) * (ds - (0.5 * ds[:, unstriped(n3)]))
    s = 0.0625 * ((x_cand.T @ mxq(z, 0, "e4m3")))
    rl = relu(s)
    ds2 = np.zeros((C, S))
    ds2[:, unstriped(n4)] = rl
    return ds2 - (0.5 * s)

@@ -1,0 +1,146 @@
+from contextlib import ExitStack
+
+import concourse.mybir as mybir
+
+K, T, S, G, H, W, C = 512, 1024, 256, 2048, 512, 128, 512
+FLOPS = 2 * K * S * (2 * H + C)
+
+F32 = mybir.dt.float32
+BF16 = mybir.dt.bfloat16
+I32 = mybir.dt.int32
+U32 = mybir.dt.uint32
+U16 = mybir.dt.uint16
+U8 = mybir.dt.uint8
+FP8X4 = mybir.dt.float8_e4m3fn_x4
+ALU = mybir.AluOpType
+COPY = mybir.ActivationFunctionType.Copy
+
+P = 128
+PACK = 4
+HALF = S // 2
+
+
+def tile_picked_aqcksetsend_none_p_kernel(tc, x_words, x_scales, d_words, d_scales, gs, offs, ka, kb, n1, n2, n3, cand, n4, out):
+    nc = tc.nc
+    with ExitStack() as ctx:
+        lists = ctx.enter_context(tc.tile_pool(name="lists", bufs=1))
+        keep = ctx.enter_context(tc.tile_pool(name="keep", bufs=1))
+        psum = ctx.enter_context(tc.psum_pool(name="psum", bufs=1))
+
+        def load_list(name, src):
+            tile = lists.tile(list(src.shape), U16, name=name)
+            nc.sync.dma_start(tile[:], src)
+            return tile
+
+        def load_words(name, src, width):
+            tile = keep.tile([P, width], U32, name=name, align_bytes=64)
+            nc.sync.dma_start(tile[:].bitcast(I32), src[0].rearrange("p n t -> p (n t)").bitcast(I32))
+            return tile
+
+        def load_scales(name, src, width):
+            tile = keep.tile([P, width], U8, name=name, align_bytes=64)
+            nc.vector.memset(tile[:].bitcast(I32), 0)
+            nc.scalar.dma_start(tile[0:P:8, :].bitcast(I32), src[0].bitcast(I32))
+            return tile
+
+        def place_scale_rows(placed, picked, queues):
+            for r in range(4):
+                queues[r % len(queues)].dma_start(placed[r:P:32, :].bitcast(I32), picked[8 * r : P : 32, :].bitcast(I32))
+
+        d_bytes = load_scales("d_bytes", d_scales, G)
+        x_bytes = load_scales("x_bytes", x_scales, T)
+        ka_t = load_list("ka_t", ka)
+        kb_t = load_list("kb_t", kb)
+        offs_t = load_list("offs_t", offs)
+        d_tab = load_words("d_tab", d_words, G)
+        x_tab = load_words("x_tab", x_words, T)
+        gs_t = keep.tile([P, PACK], F32)
+        nc.sync.dma_start(gs_t[:], gs.rearrange("(p t) o -> p (t o)", t=PACK))
+        n2_t = load_list("n2_t", n2)
+        n1_t = load_list("n1_t", n1)
+        cand_t = load_list("cand_t", cand)
+        n3_t = load_list("n3_t", n3)
+        n4_t = load_list("n4_t", n4)
+
+        gain = keep.tile([P, PACK], F32)
+        nc.scalar.activation(gain[:], gs_t[:], COPY, scale=0.0625)
+
+        placed = keep.tile([P, 2 * H + S], U8, align_bytes=64)
+        nc.vector.memset(placed[:].bitcast(I32), 0)
+        cand_placed = keep.tile([P, C], U8, align_bytes=64)
+        nc.vector.memset(cand_placed[:].bitcast(I32), 0)
+
+        picked = keep.tile([P, 2 * H + S], U8, align_bytes=64)
+        nc.vector.tensor_copy(picked[:, 0:H], d_bytes[:].indirect(ka_t[:]))
+        nc.vector.tensor_copy(picked[:, H : 2 * H], d_bytes[:].indirect(kb_t[:]))
+        nc.vector.tensor_copy(picked[:, 2 * H :], x_bytes[:].indirect(offs_t[:]))
+        place_scale_rows(placed, picked, [nc.sync, nc.scalar])
+
+        d_picked = keep.tile([P, 2 * H], U32, align_bytes=64)
+        nc.vector.tensor_copy(d_picked[:, 0:H], d_tab[:].indirect(ka_t[:]))
+        nc.vector.tensor_copy(d_picked[:, H:], d_tab[:].indirect(kb_t[:]))
+        xq = keep.tile([P, S], U32, align_bytes=64)
+        nc.vector.tensor_copy(xq[:], x_tab[:].indirect(offs_t[:]))
+
+        words_by_t = d_picked[:].rearrange("p (a m t) -> p t a m", a=2, t=PACK)
+        bytes_by_t = placed[:, 0 : 2 * H].rearrange("p (a m t) -> p t a m", a=2, t=PACK)
+        ds = []
+        for t in range(PACK):
+            w_t = keep.tile([P, 2, P], U32, name=f"w_{t}", align_bytes=64)
+            b_t = keep.tile([P, 2, P], U8, name=f"b_{t}", align_bytes=64)
+            nc.vector.tensor_copy(w_t[:], words_by_t[:, t])
+            nc.vector.tensor_copy(b_t[:], bytes_by_t[:, t])
+            acc = psum.tile([P, S], F32, name=f"h_{t}")
+            for a in range(2):
+                nc.tensor.matmul_mx(acc[:], lhsT=w_t[:, a, :].bitcast(FP8X4), lhsT_scale=b_t[:, a, :],
+                                    rhs=xq[:].bitcast(FP8X4), rhs_scale=placed[:, 2 * H :], start=(a == 0), stop=(a == 1))
+            rows = keep.tile([P, S], F32, name=f"ds_{t}")
+            if t == 0:
+                nc.scalar.activation(rows[:], acc[:], COPY, scale=gain[:, t : t + 1])
+            else:
+                nc.vector.tensor_scalar(rows[:], acc[:], gain[:, t : t + 1], None, ALU.mult)
+            ds.append(rows)
+
+        cand_picked = keep.tile([P, C], U8, align_bytes=64)
+        nc.vector.tensor_copy(cand_picked[:], x_bytes[:].indirect(cand_t[:]))
+        place_scale_rows(cand_placed, cand_picked, [nc.sync])
+        xc = keep.tile([P, C], U32, align_bytes=64)
+        nc.vector.tensor_copy(xc[:], x_tab[:].indirect(cand_t[:]))
+
+        z_planes = [keep.tile([P, PACK, HALF], BF16, name=f"z_planes_{u}", align_bytes=64) for u in range(2)]
+
+        def z_plane(u, t):
+            far = keep.tile([P, HALF], F32, name=f"far_{u}_{t}")
+            nc.scalar.activation(far[:], ds[t][:].indirect(n3_t[:, 8 * u : 8 * u + 8]), COPY)
+            nc.vector.scalar_tensor_tensor(z_planes[u][:, t, :], far[:], -0.5, ds[t][:, HALF * u : HALF * (u + 1)], ALU.mult, ALU.add)
+
+        pa = [keep.tile([P, W], F32, name=f"pa_{t}") for t in range(PACK)]
+        nc.scalar.activation(pa[0][:], ds[0][:].indirect(n2_t[:]), COPY)
+        for t in range(PACK):
+            nc.scalar.activation(ds[t][:].indirect(n1_t[:]), pa[t][:], COPY)
+            if t + 1 < PACK:
+                nc.scalar.activation(pa[t + 1][:], ds[t + 1][:].indirect(n2_t[:]), COPY)
+            z_plane(0, t)
+        for t in range(PACK):
+            z_plane(1, t)
+
+        scores = [psum.tile([P, S], F32, name=f"s_{c}") for c in range(C // P)]
+        ds2 = [keep.tile([P, S], F32, name=f"ds2_{c}") for c in range(C // P)]
+        for u in range(2):
+            cols = slice(HALF * u, HALF * (u + 1))
+            z_woven = keep.tile([P, HALF, PACK], BF16, name=f"z_woven_{u}", align_bytes=64)
+            nc.vector.tensor_copy(z_woven[:].rearrange("p (c i) t -> p c t i", i=4), z_planes[u][:].rearrange("p t (c i) -> p c t i", i=4))
+            z_codes = keep.tile([P, HALF], U32, name=f"z_codes_{u}", align_bytes=64)
+            z_scales = keep.tile([P, HALF], U8, name=f"z_scales_{u}", align_bytes=64)
+            nc.vector.quantize_mx(out=z_codes[:].bitcast(FP8X4), scales=z_scales[:], in_=z_woven[:].rearrange("p j t -> p (j t)"))
+            for c in range(C // P):
+                rows = slice(P * c, P * (c + 1))
+                nc.tensor.matmul_mx(scores[c][:, cols], lhsT=xc[:, rows].bitcast(FP8X4), lhsT_scale=cand_placed[:, rows],
+                                    rhs=z_codes[:].bitcast(FP8X4), rhs_scale=z_scales[:], start=True, stop=True)
+                rl = keep.tile([P, HALF], F32, name=f"rl_{u}_{c}")
+                nc.vector.tensor_scalar(rl[:], scores[c][:, cols], 0.0625, 0.0, ALU.mult, ALU.max)
+                nc.scalar.activation(ds2[c][:].indirect(n4_t[:, 8 * u : 8 * u + 8]), rl[:], COPY)
+        for c in range(C // P):
+            result = keep.tile([P, S], F32, name=f"result_{c}")
+            nc.vector.scalar_tensor_tensor(result[:], scores[c][:], -0.03125, ds2[c][:], ALU.mult, ALU.add)
+            nc.sync.dma_start(out[P * c : P * (c + 1), :], result[:])

@@ -17,7 +17,7 @@ COPY = mybir.ActivationFunctionType.Copy
 
 P = 128
 PACK = 4
-HALF = S // 2
+PIECES = [(0, 64), (64, 64), (128, 128)]
 
 
 def tile_picked_aqcksetsend_none_p_kernel(tc, x_words, x_scales, d_words, d_scales, gs, offs, ka, kb, n1, n2, n3, cand, n4, out):
@@ -39,27 +39,26 @@ def tile_picked_aqcksetsend_none_p_kernel(tc, x_words, x_scales, d_words, d_scal
 
         def load_scales(name, src, width):
             tile = keep.tile([P, width], U8, name=name, align_bytes=64)
-            nc.vector.memset(tile[:].bitcast(I32), 0)
-            nc.scalar.dma_start(tile[0:P:8, :].bitcast(I32), src[0].bitcast(I32))
+            nc.scalar.dma_start(tile[:].bitcast(I32), src[0].bitcast(I32).unsqueeze(1).to_broadcast([16, 8, width // 4]))
             return tile
 
         def place_scale_rows(placed, picked, queues):
             for r in range(4):
                 queues[r % len(queues)].dma_start(placed[r:P:32, :].bitcast(I32), picked[8 * r : P : 32, :].bitcast(I32))
 
-        d_bytes = load_scales("d_bytes", d_scales, G)
         x_bytes = load_scales("x_bytes", x_scales, T)
+        d_bytes = load_scales("d_bytes", d_scales, G)
+        offs_t = load_list("offs_t", offs)
         ka_t = load_list("ka_t", ka)
         kb_t = load_list("kb_t", kb)
-        offs_t = load_list("offs_t", offs)
         d_tab = load_words("d_tab", d_words, G)
-        x_tab = load_words("x_tab", x_words, T)
-        gs_t = keep.tile([P, PACK], F32)
-        nc.sync.dma_start(gs_t[:], gs.rearrange("(p t) o -> p (t o)", t=PACK))
         n2_t = load_list("n2_t", n2)
         n1_t = load_list("n1_t", n1)
-        cand_t = load_list("cand_t", cand)
+        x_tab = load_words("x_tab", x_words, T)
         n3_t = load_list("n3_t", n3)
+        gs_t = keep.tile([P, PACK], F32)
+        nc.gpsimd.dma_start(gs_t[:], gs.rearrange("(p t) o -> p (t o)", t=PACK))
+        cand_t = load_list("cand_t", cand)
         n4_t = load_list("n4_t", n4)
 
         gain = keep.tile([P, PACK], F32)
@@ -70,25 +69,27 @@ def tile_picked_aqcksetsend_none_p_kernel(tc, x_words, x_scales, d_words, d_scal
         cand_placed = keep.tile([P, C], U8, align_bytes=64)
         nc.vector.memset(cand_placed[:].bitcast(I32), 0)
 
-        picked = keep.tile([P, 2 * H + S], U8, align_bytes=64)
+        picked = keep.tile([P, 2 * H + S], U8, tag="picked_then_dealt", align_bytes=64)
+        nc.vector.tensor_copy(picked[:, 2 * H :], x_bytes[:].indirect(offs_t[:]))
         nc.vector.tensor_copy(picked[:, 0:H], d_bytes[:].indirect(ka_t[:]))
         nc.vector.tensor_copy(picked[:, H : 2 * H], d_bytes[:].indirect(kb_t[:]))
-        nc.vector.tensor_copy(picked[:, 2 * H :], x_bytes[:].indirect(offs_t[:]))
-        place_scale_rows(placed, picked, [nc.sync, nc.scalar])
+        place_scale_rows(placed, picked, [nc.scalar])
 
         d_picked = keep.tile([P, 2 * H], U32, align_bytes=64)
         nc.vector.tensor_copy(d_picked[:, 0:H], d_tab[:].indirect(ka_t[:]))
         nc.vector.tensor_copy(d_picked[:, H:], d_tab[:].indirect(kb_t[:]))
+
         xq = keep.tile([P, S], U32, align_bytes=64)
         nc.vector.tensor_copy(xq[:], x_tab[:].indirect(offs_t[:]))
-
         words_by_t = d_picked[:].rearrange("p (a m t) -> p t a m", a=2, t=PACK)
         bytes_by_t = placed[:, 0 : 2 * H].rearrange("p (a m t) -> p t a m", a=2, t=PACK)
         ds = []
+        w_first = keep.tile([P, 2, P], U32, align_bytes=64)
+        w_rest = keep.tile([P, PACK - 1, 2, P], U32, tag="picked_then_dealt", align_bytes=64)
         for t in range(PACK):
-            w_t = keep.tile([P, 2, P], U32, name=f"w_{t}", align_bytes=64)
-            b_t = keep.tile([P, 2, P], U8, name=f"b_{t}", align_bytes=64)
-            nc.vector.tensor_copy(w_t[:], words_by_t[:, t])
+            w_t = w_first[:] if t == 0 else w_rest[:, t - 1]
+            b_t = keep.tile([P, 2, P], U8, name=f"b_{t}", tag=f"b_{t}", align_bytes=64)
+            nc.vector.tensor_copy(w_t, words_by_t[:, t])
             nc.vector.tensor_copy(b_t[:], bytes_by_t[:, t])
             acc = psum.tile([P, S], F32, name=f"h_{t}")
             for a in range(2):
@@ -101,45 +102,59 @@ def tile_picked_aqcksetsend_none_p_kernel(tc, x_words, x_scales, d_words, d_scal
                 nc.vector.tensor_scalar(rows[:], acc[:], gain[:, t : t + 1], None, ALU.mult)
             ds.append(rows)
 
-        cand_picked = keep.tile([P, C], U8, align_bytes=64)
+        cand_picked = keep.tile([P, C], U8, tag=f"b_{PACK - 1}", align_bytes=64)
         nc.vector.tensor_copy(cand_picked[:], x_bytes[:].indirect(cand_t[:]))
         place_scale_rows(cand_placed, cand_picked, [nc.sync])
-        xc = keep.tile([P, C], U32, align_bytes=64)
+        xc = keep.tile([P, C], U32, tag="picked_then_dealt", align_bytes=64)
         nc.vector.tensor_copy(xc[:], x_tab[:].indirect(cand_t[:]))
 
-        z_planes = [keep.tile([P, PACK, HALF], BF16, name=f"z_planes_{u}", align_bytes=64) for u in range(2)]
+        z_planes = [keep.tile([P, PACK, n], BF16, name=f"z_planes_{j}", align_bytes=64) for j, n in PIECES[:-1]]
 
-        def z_plane(u, t):
-            far = keep.tile([P, HALF], F32, name=f"far_{u}_{t}")
-            nc.scalar.activation(far[:], ds[t][:].indirect(n3_t[:, 8 * u : 8 * u + 8]), COPY)
-            nc.vector.scalar_tensor_tensor(z_planes[u][:, t, :], far[:], -0.5, ds[t][:, HALF * u : HALF * (u + 1)], ALU.mult, ALU.add)
+        def z_plane(u, t, far):
+            j, n = PIECES[u]
+            nc.scalar.activation(far, ds[t][:].indirect(n3_t[:, j // 16 : (j + n) // 16]), COPY)
+            nc.vector.scalar_tensor_tensor(z_planes[u][:, t, :], far, -0.5, ds[t][:, j : j + n], ALU.mult, ALU.add)
 
-        pa = [keep.tile([P, W], F32, name=f"pa_{t}") for t in range(PACK)]
+        first = PIECES[0][1]
+        pa = [keep.tile([P, W], F32, name=f"pa_{t}", tag=f"pa_{t}") for t in range(PACK)]
+        far_first = keep.tile([P, PACK, first], F32)
         nc.scalar.activation(pa[0][:], ds[0][:].indirect(n2_t[:]), COPY)
         for t in range(PACK):
             nc.scalar.activation(ds[t][:].indirect(n1_t[:]), pa[t][:], COPY)
             if t + 1 < PACK:
                 nc.scalar.activation(pa[t + 1][:], ds[t + 1][:].indirect(n2_t[:]), COPY)
-            z_plane(0, t)
-        for t in range(PACK):
-            z_plane(1, t)
+            z_plane(0, t, far_first[:, t, :])
+        far_rest = keep.tile([P, PACK, S - first], F32, tag=f"pa_{PACK - 1}")
 
         scores = [psum.tile([P, S], F32, name=f"s_{c}") for c in range(C // P)]
         ds2 = [keep.tile([P, S], F32, name=f"ds2_{c}") for c in range(C // P)]
-        for u in range(2):
-            cols = slice(HALF * u, HALF * (u + 1))
-            z_woven = keep.tile([P, HALF, PACK], BF16, name=f"z_woven_{u}", align_bytes=64)
+
+        def score(u):
+            j, n = PIECES[u]
+            z_woven = keep.tile([P, n, PACK], BF16, name=f"z_woven_{u}", align_bytes=64)
             nc.vector.tensor_copy(z_woven[:].rearrange("p (c i) t -> p c t i", i=4), z_planes[u][:].rearrange("p t (c i) -> p c t i", i=4))
-            z_codes = keep.tile([P, HALF], U32, name=f"z_codes_{u}", align_bytes=64)
-            z_scales = keep.tile([P, HALF], U8, name=f"z_scales_{u}", align_bytes=64)
+            z_codes = keep.tile([P, n], U32, name=f"z_codes_{u}", tag=f"z_codes_{u}", align_bytes=64)
+            z_scales = keep.tile([P, n], U8, name=f"z_scales_{u}", align_bytes=64)
             nc.vector.quantize_mx(out=z_codes[:].bitcast(FP8X4), scales=z_scales[:], in_=z_woven[:].rearrange("p j t -> p (j t)"))
             for c in range(C // P):
                 rows = slice(P * c, P * (c + 1))
-                nc.tensor.matmul_mx(scores[c][:, cols], lhsT=xc[:, rows].bitcast(FP8X4), lhsT_scale=cand_placed[:, rows],
+                nc.tensor.matmul_mx(scores[c][:, j : j + n], lhsT=xc[:, rows].bitcast(FP8X4), lhsT_scale=cand_placed[:, rows],
                                     rhs=z_codes[:].bitcast(FP8X4), rhs_scale=z_scales[:], start=True, stop=True)
-                rl = keep.tile([P, HALF], F32, name=f"rl_{u}_{c}")
-                nc.vector.tensor_scalar(rl[:], scores[c][:, cols], 0.0625, 0.0, ALU.mult, ALU.max)
-                nc.scalar.activation(ds2[c][:].indirect(n4_t[:, 8 * u : 8 * u + 8]), rl[:], COPY)
+                rl = keep.tile([P, n], F32, name=f"rl_{u}_{c}")
+                nc.vector.tensor_scalar(rl[:], scores[c][:, j : j + n], 0.0625, 0.0, ALU.mult, ALU.max)
+                positive.append((c, j, n, rl))
+
+        positive = []
+        score(0)
+        for u in range(1, len(PIECES)):
+            j, n = PIECES[u]
+            if u == len(PIECES) - 1:
+                z_planes.append(keep.tile([P, PACK, n], BF16, name="z_planes_last", tag="z_codes_0", align_bytes=64))
+            for t in range(PACK):
+                z_plane(u, t, far_rest[:, t, j - first : j - first + n])
+            score(u)
+        for c, j, n, rl in positive:
+            nc.scalar.activation(ds2[c][:].indirect(n4_t[:, j // 16 : (j + n) // 16]), rl[:], COPY)
         for c in range(C // P):
             result = keep.tile([P, S], F32, name=f"result_{c}")
             nc.vector.scalar_tensor_tensor(result[:], scores[c][:], -0.03125, ds2[c][:], ALU.mult, ALU.add)

from contextlib import ExitStack

import concourse.mybir as mybir

K, T, S, G, H, W, C = 512, 1024, 256, 2048, 512, 128, 512
FLOPS = 2 * K * S * (2 * H + C)

F32 = mybir.dt.float32
BF16 = mybir.dt.bfloat16
I32 = mybir.dt.int32
U32 = mybir.dt.uint32
U16 = mybir.dt.uint16
U8 = mybir.dt.uint8
FP8X4 = mybir.dt.float8_e4m3fn_x4
ALU = mybir.AluOpType
COPY = mybir.ActivationFunctionType.Copy

P = 128
PACK = 4
PIECES = [(0, 64), (64, 64), (128, 128)]


def tile_picked_aqcksetsend_none_p_kernel(tc, x_words, x_scales, d_words, d_scales, gs, offs, ka, kb, n1, n2, n3, cand, n4, out):
    nc = tc.nc
    with ExitStack() as ctx:
        lists = ctx.enter_context(tc.tile_pool(name="lists", bufs=1))
        keep = ctx.enter_context(tc.tile_pool(name="keep", bufs=1))
        psum = ctx.enter_context(tc.psum_pool(name="psum", bufs=1))

        def load_list(name, src):
            tile = lists.tile(list(src.shape), U16, name=name)
            nc.sync.dma_start(tile[:], src)
            return tile

        def load_words(name, src, width):
            tile = keep.tile([P, width], U32, name=name, align_bytes=64)
            nc.sync.dma_start(tile[:].bitcast(I32), src[0].rearrange("p n t -> p (n t)").bitcast(I32))
            return tile

        def load_scales(name, src, width):
            tile = keep.tile([P, width], U8, name=name, align_bytes=64)
            nc.scalar.dma_start(tile[:].bitcast(I32), src[0].bitcast(I32).unsqueeze(1).to_broadcast([16, 8, width // 4]))
            return tile

        def place_scale_rows(placed, picked, queues):
            for r in range(4):
                queues[r % len(queues)].dma_start(placed[r:P:32, :].bitcast(I32), picked[8 * r : P : 32, :].bitcast(I32))

        x_bytes = load_scales("x_bytes", x_scales, T)
        d_bytes = load_scales("d_bytes", d_scales, G)
        offs_t = load_list("offs_t", offs)
        ka_t = load_list("ka_t", ka)
        kb_t = load_list("kb_t", kb)
        d_tab = load_words("d_tab", d_words, G)
        n2_t = load_list("n2_t", n2)
        n1_t = load_list("n1_t", n1)
        x_tab = load_words("x_tab", x_words, T)
        n3_t = load_list("n3_t", n3)
        gs_t = keep.tile([P, PACK], F32)
        nc.gpsimd.dma_start(gs_t[:], gs.rearrange("(p t) o -> p (t o)", t=PACK))
        cand_t = load_list("cand_t", cand)
        n4_t = load_list("n4_t", n4)

        gain = keep.tile([P, PACK], F32)
        nc.scalar.activation(gain[:], gs_t[:], COPY, scale=0.0625)

        placed = keep.tile([P, 2 * H + S], U8, align_bytes=64)
        nc.vector.memset(placed[:].bitcast(I32), 0)
        cand_placed = keep.tile([P, C], U8, align_bytes=64)
        nc.vector.memset(cand_placed[:].bitcast(I32), 0)

        picked = keep.tile([P, 2 * H + S], U8, tag="picked_then_dealt", align_bytes=64)
        nc.vector.tensor_copy(picked[:, 2 * H :], x_bytes[:].indirect(offs_t[:]))
        nc.vector.tensor_copy(picked[:, 0:H], d_bytes[:].indirect(ka_t[:]))
        nc.vector.tensor_copy(picked[:, H : 2 * H], d_bytes[:].indirect(kb_t[:]))
        place_scale_rows(placed, picked, [nc.scalar])

        d_picked = keep.tile([P, 2 * H], U32, align_bytes=64)
        nc.vector.tensor_copy(d_picked[:, 0:H], d_tab[:].indirect(ka_t[:]))
        nc.vector.tensor_copy(d_picked[:, H:], d_tab[:].indirect(kb_t[:]))

        xq = keep.tile([P, S], U32, align_bytes=64)
        nc.vector.tensor_copy(xq[:], x_tab[:].indirect(offs_t[:]))
        words_by_t = d_picked[:].rearrange("p (a m t) -> p t a m", a=2, t=PACK)
        bytes_by_t = placed[:, 0 : 2 * H].rearrange("p (a m t) -> p t a m", a=2, t=PACK)
        ds = []
        w_first = keep.tile([P, 2, P], U32, align_bytes=64)
        w_rest = keep.tile([P, PACK - 1, 2, P], U32, tag="picked_then_dealt", align_bytes=64)
        for t in range(PACK):
            w_t = w_first[:] if t == 0 else w_rest[:, t - 1]
            b_t = keep.tile([P, 2, P], U8, name=f"b_{t}", tag=f"b_{t}", align_bytes=64)
            nc.vector.tensor_copy(w_t, words_by_t[:, t])
            nc.vector.tensor_copy(b_t[:], bytes_by_t[:, t])
            acc = psum.tile([P, S], F32, name=f"h_{t}")
            for a in range(2):
                nc.tensor.matmul_mx(acc[:], lhsT=w_t[:, a, :].bitcast(FP8X4), lhsT_scale=b_t[:, a, :],
                                    rhs=xq[:].bitcast(FP8X4), rhs_scale=placed[:, 2 * H :], start=(a == 0), stop=(a == 1))
            rows = keep.tile([P, S], F32, name=f"ds_{t}")
            if t == 0:
                nc.scalar.activation(rows[:], acc[:], COPY, scale=gain[:, t : t + 1])
            else:
                nc.vector.tensor_scalar(rows[:], acc[:], gain[:, t : t + 1], None, ALU.mult)
            ds.append(rows)

        cand_picked = keep.tile([P, C], U8, tag=f"b_{PACK - 1}", align_bytes=64)
        nc.vector.tensor_copy(cand_picked[:], x_bytes[:].indirect(cand_t[:]))
        place_scale_rows(cand_placed, cand_picked, [nc.sync])
        xc = keep.tile([P, C], U32, tag="picked_then_dealt", align_bytes=64)
        nc.vector.tensor_copy(xc[:], x_tab[:].indirect(cand_t[:]))

        z_planes = [keep.tile([P, PACK, n], BF16, name=f"z_planes_{j}", align_bytes=64) for j, n in PIECES[:-1]]

        def z_plane(u, t, far):
            j, n = PIECES[u]
            nc.scalar.activation(far, ds[t][:].indirect(n3_t[:, j // 16 : (j + n) // 16]), COPY)
            nc.vector.scalar_tensor_tensor(z_planes[u][:, t, :], far, -0.5, ds[t][:, j : j + n], ALU.mult, ALU.add)

        first = PIECES[0][1]
        pa = [keep.tile([P, W], F32, name=f"pa_{t}", tag=f"pa_{t}") for t in range(PACK)]
        far_first = keep.tile([P, PACK, first], F32)
        nc.scalar.activation(pa[0][:], ds[0][:].indirect(n2_t[:]), COPY)
        for t in range(PACK):
            nc.scalar.activation(ds[t][:].indirect(n1_t[:]), pa[t][:], COPY)
            if t + 1 < PACK:
                nc.scalar.activation(pa[t + 1][:], ds[t + 1][:].indirect(n2_t[:]), COPY)
            z_plane(0, t, far_first[:, t, :])
        far_rest = keep.tile([P, PACK, S - first], F32, tag=f"pa_{PACK - 1}")

        scores = [psum.tile([P, S], F32, name=f"s_{c}") for c in range(C // P)]
        ds2 = [keep.tile([P, S], F32, name=f"ds2_{c}") for c in range(C // P)]

        def score(u):
            j, n = PIECES[u]
            z_woven = keep.tile([P, n, PACK], BF16, name=f"z_woven_{u}", align_bytes=64)
            nc.vector.tensor_copy(z_woven[:].rearrange("p (c i) t -> p c t i", i=4), z_planes[u][:].rearrange("p t (c i) -> p c t i", i=4))
            z_codes = keep.tile([P, n], U32, name=f"z_codes_{u}", tag=f"z_codes_{u}", align_bytes=64)
            z_scales = keep.tile([P, n], U8, name=f"z_scales_{u}", align_bytes=64)
            nc.vector.quantize_mx(out=z_codes[:].bitcast(FP8X4), scales=z_scales[:], in_=z_woven[:].rearrange("p j t -> p (j t)"))
            for c in range(C // P):
                rows = slice(P * c, P * (c + 1))
                nc.tensor.matmul_mx(scores[c][:, j : j + n], lhsT=xc[:, rows].bitcast(FP8X4), lhsT_scale=cand_placed[:, rows],
                                    rhs=z_codes[:].bitcast(FP8X4), rhs_scale=z_scales[:], start=True, stop=True)
                rl = keep.tile([P, n], F32, name=f"rl_{u}_{c}")
                nc.vector.tensor_scalar(rl[:], scores[c][:, j : j + n], 0.0625, 0.0, ALU.mult, ALU.max)
                positive.append((c, j, n, rl))

        positive = []
        score(0)
        for u in range(1, len(PIECES)):
            j, n = PIECES[u]
            if u == len(PIECES) - 1:
                z_planes.append(keep.tile([P, PACK, n], BF16, name="z_planes_last", tag="z_codes_0", align_bytes=64))
            for t in range(PACK):
                z_plane(u, t, far_rest[:, t, j - first : j - first + n])
            score(u)
        for c, j, n, rl in positive:
            nc.scalar.activation(ds2[c][:].indirect(n4_t[:, j // 16 : (j + n) // 16]), rl[:], COPY)
        for c in range(C // P):
            result = keep.tile([P, S], F32, name=f"result_{c}")
            nc.vector.scalar_tensor_tensor(result[:], scores[c][:], -0.03125, ds2[c][:], ALU.mult, ALU.add)
            nc.sync.dma_start(out[P * c : P * (c + 1), :], result[:])
